import numpy as np
import ml_dtypes


def mxq(x, axis, fmt="e4m3"):
    dtype, down = {"e4m3": (ml_dtypes.float8_e4m3fn, 7), "e5m2": (ml_dtypes.float8_e5m2, 14)}[fmt]
    v = np.moveaxis(np.asarray(x, np.float32).astype(ml_dtypes.bfloat16).astype(np.float64), axis, -1)
    blocks = v.reshape(v.shape[:-1] + (-1, 32))
    amax = np.abs(blocks).max(-1, keepdims=True)
    byte = np.maximum(np.where(amax > 0, np.frexp(amax)[1] - 1 + 127, 0) - down, 1)
    scale = np.exp2(byte - 127.0)
    codes = (blocks / scale).astype(np.float32).astype(dtype).astype(np.float64)
    return np.moveaxis((codes * scale).reshape(v.shape), -1, axis)


WIDE = False


def mx_kscale(k):
    if not WIDE:
        return np.ones(k)
    levels = np.array([10, -10, 5, -5, 0])
    if k % 512:
        return np.exp2(np.random.permutation(np.resize(levels, k // 32))).repeat(32)
    a = np.empty((k // 512, 16))
    for p in range(k // 512):
        a[p, :8] = np.random.permutation(np.resize(levels, 8))
        for g in range(8):
            far = levels[np.abs(levels - a[p, g]) >= 10]
            a[p, g + 8] = far[np.random.randint(len(far))]
    return np.exp2(a.ravel()).repeat(32)


def f64(x):
    return np.asarray(x).astype(np.float64)


def striped(idx):
    return np.tile(idx.reshape(-1, 16).T, (8, 1)).astype(np.uint16)


def unstriped(offs):
    return offs[:16].T.reshape(-1).astype(np.int64)


def striped8(idx):
    return np.concatenate([x.reshape(-1, 16).T for x in idx]).astype(np.uint16)


def runs(offs, k):
    lists = np.stack([offs[16 * r : 16 * r + 16].T.reshape(-1) for r in range(8)]).astype(np.int64)
    return lists[np.arange(k) % 512 // 64]


def pack_weight(w):
    k, n = w.shape
    w = f64(np.asarray(w, np.float32).astype(ml_dtypes.bfloat16)).reshape(k // 32, 32, n)
    amax = np.abs(w).max(1)
    byte = np.clip(np.where(amax > 0, np.frexp(amax)[1] - 1 + 127 - 7, 1), 1, 254)
    scaled = (w * np.exp2(127.0 - byte)[:, None, :]).reshape(k, n).astype(np.float32)
    words = np.ascontiguousarray(scaled.reshape(k // 512, 128, 4, n).transpose(0, 1, 3, 2)).astype(ml_dtypes.float8_e4m3fn).view(np.uint8)
    return words, np.ascontiguousarray(byte.astype(np.uint8).reshape(k // 512, 16, n))


def unpack_weight(words, scales):
    g, p, n, _ = words.shape
    vals = np.ascontiguousarray(words).view(ml_dtypes.float8_e4m3fn).astype(np.float64) * np.repeat(np.exp2(scales.astype(np.float64) - 127.0), 8, axis=1)[..., None]
    return vals.transpose(0, 1, 3, 2).reshape(g * 512, n)


def sigmoid(v):
    return 1.0 / (1.0 + np.exp(-np.maximum(v, -700.0)))

def planes(y):
    n, m = y.shape
    v = y.astype(np.float32).astype(ml_dtypes.bfloat16).astype(np.float64).reshape(n // 32, 32, m)
    top = np.abs(v).max(1)
    byte = np.clip(np.where(top > 0, np.frexp(top)[1] - 1 + 127 - 7, 1), 1, 254)
    codes = (v * np.exp2(127.0 - byte)[:, None, :]).reshape(n, m).astype(np.float32).astype(ml_dtypes.float8_e4m3fn).view(np.uint8)
    words = codes.reshape(n // 512, 128, 4, m).transpose(0, 1, 3, 2)
    return np.ascontiguousarray(words), np.ascontiguousarray(byte.astype(np.uint8).reshape(n // 512, 16, m))


K, T, S, H, C = 512, 2048, 256, 512, 512


def setup_inputs():
    n = np.random.standard_normal
    s = mx_kscale(K)[:, None]
    packed_xT = pack_weight(n((K, T)) * s)
    packed_w1 = pack_weight(n((K, H)) / np.sqrt(K) / s)
    return {
        "x_words": packed_xT[0],
        "x_scales": packed_xT[1],
        "w1_words": packed_w1[0],
        "w1_scales": packed_w1[1],
        "sl": np.random.uniform(1.0, 2.0, (H, 1)).astype(np.float32),
        "th": (0.5 * n((H, 1))).astype(np.float32),
        "gs": (np.random.uniform(0.5, 1.5, (K, 1)) / s).astype(np.float32),
        "tau": np.random.uniform(0.3, 0.9, (C, 1)).astype(np.float32),
        "sl2": np.random.uniform(1.0, 2.0, (C, 1)).astype(np.float32),
        "th2": (0.5 * n((C, 1))).astype(np.float32),
        "offs": striped(np.random.permutation(T)[:S]),
        "n1": striped8(np.stack([np.random.permutation(S) for _ in range(8)])),
        "n2": striped8(np.stack([np.random.permutation(S) for _ in range(8)])),
        "ca": striped(np.random.permutation(T)[:C]),
        "cb": striped(np.random.permutation(T)[:C]),
        "cd": striped(np.random.permutation(T)[:C]),
        "n3": striped(np.random.permutation(S)),
        "n4": striped(np.random.permutation(S)),
        "n5": striped(np.random.permutation(S)),
        "n6": striped(np.random.permutation(S)),
    }


def reference(x_words, x_scales, w1_words, w1_scales, sl, th, gs, tau, sl2, th2, offs, n1, n2, ca, cb, cd, n3, n4, n5, n6):
    x_ca = unpack_weight(x_words, x_scales)[:, unstriped(ca)]
    xq = unpack_weight(x_words, x_scales)[:, unstriped(offs)]
    y = unpack_weight(w1_words, w1_scales).T @ xq
    sg = sigmoid(f64(sl) * (y[np.arange(H)[:, None], runs(n1, H)] - f64(th)))
    st = y * sg
    z = f64(gs) * (st - (0.5 * (st[np.arange(H)[:, None], runs(n2, H)])))
    zq = mxq(z, 0, "e4m3")
    a = 0.0625 * (x_ca.T @ zq)
    x_cb = unpack_weight(x_words, x_scales)[:, unstriped(cb)]
    b = 0.0625 * (x_cb.T @ zq)
    top = b.max(axis=1, keepdims=True)
    ea = np.exp(f64(tau) * (b[:, unstriped(n3)] - top))
    m1 = (0.5 * (a - a[:, unstriped(n4)])) / (ea + 0.25)
    x_cd = unpack_weight(x_words, x_scales)[:, unstriped(cd)]
    q = 0.0625 * (x_cd.T @ zq)
    sg2 = sigmoid(f64(sl2) * (q[:, unstriped(n5)] - f64(th2)))
    out_0 = m1 * sg2 - (0.5 * m1[:, unstriped(n6)])
    return (out_0,) + planes(out_0)

@@ -1,0 +1,227 @@
+from contextlib import ExitStack
+
+import concourse.mybir as mybir
+
+K, T, S, H, C = 512, 2048, 256, 512, 512
+FLOPS = 2 * K * S * (H + 3 * C)
+
+F32 = mybir.dt.float32
+BF16 = mybir.dt.bfloat16
+I32 = mybir.dt.int32
+U32 = mybir.dt.uint32
+U16 = mybir.dt.uint16
+U8 = mybir.dt.uint8
+FP8X4 = mybir.dt.float8_e4m3fn_x4
+ACT = mybir.ActivationFunctionType
+ALU = mybir.AluOpType
+
+P = 128
+PACK = 4
+HALF = S // 2
+HALF_LIST = HALF // 16
+
+
+def tile_picked_tricdqxbgxbehp_none_po_kernel(
+    tc, x_words, x_scales, w1_words, w1_scales, sl, th, gs, tau, sl2, th2,
+    offs, n1, n2, ca, cb, cd, n3, n4, n5, n6, out_0, out_1, out_2,
+):
+    nc = tc.nc
+    with ExitStack() as ctx:
+        pool = ctx.enter_context(tc.tile_pool(name="sb", bufs=1))
+        psum = ctx.enter_context(tc.psum_pool(name="ps", bufs=1))
+
+        def sb(name, shape, dtype, tag=None):
+            return pool.tile(shape, dtype, name=name, tag=tag or name, align_bytes=64)
+
+        def load_list(name, src):
+            t = sb(name, list(src.shape), U16)
+            nc.sync.dma_start(t[:], src)
+            return t
+
+        def load_rows(name, src, eng):
+            t = sb(name, [P, PACK], F32)
+            eng.dma_start(t[:], src.rearrange("(p t) o -> p (t o)", t=PACK))
+            return t
+
+        def load_scales(t, src, engs):
+            for q, eng in enumerate(engs):
+                eng.dma_start(t[32 * q : 32 * q + 4, :].bitcast(I32), src[0, 4 * q : 4 * q + 4, :].bitcast(I32))
+
+        def half(t, h):
+            return t[:, h * HALF_LIST : (h + 1) * HALF_LIST]
+
+        xw = sb("xw", [P, T], U32)
+        xs = sb("xs", [P, T], U8)
+        ww = sb("ww", [P, H], U32)
+        ws = sb("ws", [P, H], U8)
+        nc.gpsimd.memset(ws[:].bitcast(I32), 0)
+        nc.gpsimd.memset(xs[:].bitcast(I32), 0)
+        offs_t = load_list("offs", offs)
+        nc.sync.dma_start(xw[:].bitcast(I32), x_words[0].rearrange("p n r -> p (n r)").bitcast(I32))
+        load_scales(ws, w1_scales, [nc.scalar] * 4)
+        load_scales(xs, x_scales, [nc.scalar] * 3 + [nc.gpsimd])
+        nc.sync.dma_start(ww[:].bitcast(I32), w1_words[0].rearrange("p n r -> p (n r)").bitcast(I32))
+        sl_t = load_rows("sl", sl, nc.gpsimd)
+        th_t = load_rows("th", th, nc.sync)
+        n1_t = load_list("n1", n1)
+        cb_t = load_list("cb", cb)
+        gs_t = load_rows("gs", gs, nc.gpsimd)
+        cd_t = load_list("cd", cd)
+        n2_t = load_list("n2", n2)
+        ca_t = load_list("ca", ca)
+        tau_t = load_rows("tau", tau, nc.sync)
+        sl2_t = load_rows("sl2", sl2, nc.sync)
+        th2_t = load_rows("th2", th2, nc.sync)
+        n3_t = load_list("n3", n3)
+        n4_t = load_list("n4", n4)
+        n5_t = load_list("n5", n5)
+        n6_t = load_list("n6", n6)
+
+        wsd = sb("wsd", [P, H], U8)
+        nc.vector.tensor_copy(
+            wsd[:].rearrange("p (t m) -> p m t", t=PACK), ws[:].rearrange("p (m t) -> p m t", t=PACK)
+        )
+
+        xqw = sb("xqw", [P, S], U32)
+        xqs = sb("xqs", [P, S], U8)
+        nc.vector.tensor_copy(xqw[:], xw[:].indirect(offs_t[:]))
+        nc.vector.tensor_copy(xqs[:], xs[:].indirect(offs_t[:]))
+
+        wwd = sb("wwd", [P, H], U32)
+        nc.vector.tensor_copy(
+            wwd[:].rearrange("p (t g i) -> p g t i", t=PACK, i=4),
+            ww[:].rearrange("p (g i t) -> p g t i", t=PACK, i=4),
+        )
+        nb1 = sb("nb1", [P, PACK], F32)
+        nb0 = sb("nb0", [P, 1], F32, "y1")
+        nc.vector.scalar_tensor_tensor(nb0[:], sl_t[:, :1], -1.0, th_t[:, :1], ALU.mult, ALU.mult)
+        nc.vector.scalar_tensor_tensor(nb1[:, 1:], sl_t[:, 1:], -1.0, th_t[:, 1:], ALU.mult, ALU.mult)
+
+        def pick(name, lst, wtag=None, stag=None):
+            w = sb(name + "w", [P, C], U32, wtag)
+            s = sb(name + "s", [P, C], U8, stag)
+            nc.vector.tensor_copy(w[:].rearrange("p (t m) -> p m t", t=PACK), xw[:].indirect(lst[:]))
+            nc.vector.tensor_copy(s[:].rearrange("p (t m) -> p m t", t=PACK), xs[:].indirect(lst[:]))
+            return w, s
+
+        def mm(out, lhs, t, rhs):
+            cols = slice(t * P, (t + 1) * P)
+            nc.tensor.matmul_mx(
+                out, lhsT=lhs[0][:, cols].bitcast(FP8X4), lhsT_scale=lhs[1][:, cols],
+                rhs=rhs[0][:].bitcast(FP8X4), rhs_scale=rhs[1][:], start=True, stop=True,
+            )
+
+        st_t, bg_t = [], []
+        for t in range(PACK):
+            py = psum.tile([P, S], F32, name=f"pn{t}")
+            mm(py[:], (wwd, wsd), t, (xqw, xqs))
+            y = sb(f"y{t}", [P, S], F32)
+            move = nc.scalar.copy if t else nc.vector.tensor_copy
+            move(y[:], py[:])
+            st = sb(f"st{t}", [P, 2 * S], F32)
+            for h in range(2):
+                nc.scalar.activation(
+                    st[:, S + h * HALF : S + (h + 1) * HALF], y[:].indirect(half(n1_t, h)), ACT.Sigmoid,
+                    bias=nb1[:, t : t + 1] if t else nb0[:], scale=sl_t[:, t : t + 1],
+                )
+            nc.vector.scalar_tensor_tensor(st[:, :S], py[:], gs_t[:, t : t + 1], st[:, S:], ALU.mult, ALU.mult)
+            st_t.append(st)
+            bg_t.append(sb(f"bg{t}", [P, 2 * S], F32))
+
+        xb = pick("xb", cb_t)
+        zw = sb("zw", [P, S], U32)
+        zs = sb("zs", [P, S], U8)
+        for h in range(2):
+            cols = slice(h * HALF, (h + 1) * HALF)
+            zb = sb(f"zb{h}", [P, PACK, HALF], BF16)
+            for t in range(PACK):
+                g = bg_t[t][:, S + h * HALF : S + (h + 1) * HALF]
+                nc.scalar.activation(g, st_t[t][:].indirect(half(n2_t, h)), ACT.Copy)
+                nc.vector.scalar_tensor_tensor(zb[:, t, :], g, -0.5, st_t[t][:, cols], ALU.mult, ALU.add)
+            zi = sb(f"zi{h}", [P, HALF * PACK], BF16)
+            nc.vector.tensor_copy(
+                zi[:].rearrange("p (c i t) -> p c t i", t=PACK, i=4),
+                zb[:].rearrange("p t (c i) -> p c t i", i=4),
+            )
+            nc.vector.quantize_mx(zw[:, cols].bitcast(FP8X4), zs[:, cols], zi[:])
+
+        xd = pick("xd", cd_t, "y1", "y3")
+
+        ea = sb("ea", [P, PACK * S], F32)
+        nb3 = sb("nb3", [P, PACK], F32)
+        for t in range(PACK):
+            pb = psum.tile([P, S], F32, name=f"pw{t}")
+            mm(pb[:], xb, t, (zw, zs))
+            top = sb(f"top{t}", [P, 1], F32)
+            nc.vector.tensor_scalar(bg_t[t][:, :S], pb[:], 0.0625, None, ALU.mult, ALU.max, accum_out=top[:])
+            nc.vector.tensor_scalar(nb3[:, t : t + 1], top[:], tau_t[:, t : t + 1], -1.0, ALU.mult, ALU.mult)
+            nc.scalar.activation(
+                ea[:, t * S : (t + 1) * S], bg_t[t][:].indirect(n3_t[:]), ACT.Exp,
+                bias=nb3[:, t : t + 1], scale=tau_t[:, t : t + 1],
+            )
+        xa = pick("xa", ca_t, "zi1", "top3")
+        nb5 = sb("nb5", [P, PACK], F32)
+        nc.vector.scalar_tensor_tensor(nb5[:], sl2_t[:], -1.0, th2_t[:], ALU.mult, ALU.mult)
+
+        rs = sb("rs", [P, PACK * S], F32)
+        nc.scalar.activation(rs[:], ea[:], ACT.Abs_reciprocal_sqrt, bias=0.25)
+
+        for t in range(PACK):
+            pq = psum.tile([P, S], F32, name=f"pn{t}")
+            mm(pq[:], xd, t, (zw, zs))
+            nc.scalar.activation(bg_t[t][:, :S], pq[:], ACT.Copy, scale=0.0625)
+
+        d_t = []
+        for t in range(PACK):
+            pa = psum.tile([P, S], F32, name=f"pw{t}")
+            mm(pa[:], xa, t, (zw, zs))
+            nc.vector.tensor_scalar(st_t[t][:, :S], pa[:], 0.0625, None, ALU.mult)
+            ga = sb(f"ga{t}", [P, S], F32)
+            nc.vector.tensor_copy(ga[:], st_t[t][:].indirect(n4_t[:]))
+            d = sb(f"d{t}", [P, S], F32)
+            nc.vector.scalar_tensor_tensor(d[:], pa[:], 0.0625, ga[:], ALU.mult, ALU.subtract)
+            d_t.append(d)
+        for t in range(PACK):
+            cols = slice(t * S, (t + 1) * S)
+            nc.scalar.activation(
+                ea[:, cols], bg_t[t][:].indirect(n5_t[:]), ACT.Sigmoid,
+                bias=nb5[:, t : t + 1], scale=sl2_t[:, t : t + 1],
+            )
+        hm_t = []
+        for t in range(PACK):
+            cols = slice(t * S, (t + 1) * S)
+            hm = sb(f"hm{t}", [P, 2 * S], F32)
+            nc.vector.scalar_tensor_tensor(hm[:, S:], d_t[t][:], -0.25, rs[:, cols], ALU.mult, ALU.mult)
+            nc.vector.tensor_tensor(hm[:, :S], hm[:, S:], rs[:, cols], ALU.mult)
+            hm_t.append(hm)
+
+        o = sb("o", [P, PACK, S], F32)
+        out_rows = out_0.rearrange("(p t) j -> p t j", t=PACK)
+        for t in range(PACK):
+            cols = slice(t * S, (t + 1) * S)
+            p = sb(f"p{t}", [P, S], F32)
+            nc.vector.scalar_tensor_tensor(p[:], hm_t[t][:, :S], -2.0, ea[:, cols], ALU.mult, ALU.mult)
+            if t < 2:
+                g6 = sb(f"g6{t}", [P, S], F32)
+                nc.scalar.activation(g6[:], hm_t[t][:].indirect(n6_t[:]), ACT.Copy)
+                nc.vector.tensor_tensor(o[:, t, :], g6[:], p[:], ALU.add)
+            else:
+                nc.vector.tensor_tensor(o[:, t, :], hm_t[t][:].indirect(n6_t[:]), p[:], ALU.add)
+            nc.sync.dma_start(out_rows[:, t, :], o[:, t, :])
+
+        ow = sb("ow", [P, S], U32)
+        osc = sb("osc", [P, S], U8)
+        out_words = out_1[0].rearrange("p n r -> p (n r)").bitcast(I32)
+        for h in range(2):
+            cols = slice(h * HALF, (h + 1) * HALF)
+            oi = sb(f"oi{h}", [P, HALF * PACK], BF16)
+            move = nc.scalar.copy if h else nc.vector.tensor_copy
+            move(
+                oi[:].rearrange("p (c i t) -> p c t i", t=PACK, i=4),
+                o[:, :, cols].rearrange("p t (c i) -> p c t i", i=4),
+            )
+            nc.vector.quantize_mx(ow[:, cols].bitcast(FP8X4), osc[:, cols], oi[:])
+        nc.sync.dma_start(out_words, ow[:].bitcast(I32))
+        for q in range(4):
+            eng = nc.sync if q % 2 else nc.scalar
+            eng.dma_start(out_2[0, 4 * q : 4 * q + 4, :].bitcast(I32), osc[32 * q : 32 * q + 4, :].bitcast(I32))

@@ -58,17 +58,17 @@ def tile_picked_tricdqxbgxbehp_none_po_kernel(
         nc.gpsimd.memset(xs[:].bitcast(I32), 0)
         offs_t = load_list("offs", offs)
         nc.sync.dma_start(xw[:].bitcast(I32), x_words[0].rearrange("p n r -> p (n r)").bitcast(I32))
-        load_scales(ws, w1_scales, [nc.scalar] * 4)
-        load_scales(xs, x_scales, [nc.scalar] * 3 + [nc.gpsimd])
+        load_scales(ws, w1_scales, [nc.scalar] * 3 + [nc.gpsimd])
+        load_scales(xs, x_scales, [nc.scalar] * 4)
         nc.sync.dma_start(ww[:].bitcast(I32), w1_words[0].rearrange("p n r -> p (n r)").bitcast(I32))
-        sl_t = load_rows("sl", sl, nc.gpsimd)
-        th_t = load_rows("th", th, nc.sync)
         n1_t = load_list("n1", n1)
+        sl_t = load_rows("sl", sl, nc.sync)
+        th_t = load_rows("th", th, nc.sync)
         cb_t = load_list("cb", cb)
         gs_t = load_rows("gs", gs, nc.gpsimd)
         cd_t = load_list("cd", cd)
-        n2_t = load_list("n2", n2)
         ca_t = load_list("ca", ca)
+        n2_t = load_list("n2", n2)
         tau_t = load_rows("tau", tau, nc.sync)
         sl2_t = load_rows("sl2", sl2, nc.sync)
         th2_t = load_rows("th2", th2, nc.sync)
@@ -92,17 +92,22 @@ def tile_picked_tricdqxbgxbehp_none_po_kernel(
             wwd[:].rearrange("p (t g i) -> p g t i", t=PACK, i=4),
             ww[:].rearrange("p (g i t) -> p g t i", t=PACK, i=4),
         )
-        nb1 = sb("nb1", [P, PACK], F32)
-        nb0 = sb("nb0", [P, 1], F32, "y1")
-        nc.vector.scalar_tensor_tensor(nb0[:], sl_t[:, :1], -1.0, th_t[:, :1], ALU.mult, ALU.mult)
-        nc.vector.scalar_tensor_tensor(nb1[:, 1:], sl_t[:, 1:], -1.0, th_t[:, 1:], ALU.mult, ALU.mult)
+        def gate_bias(name, slope, threshold):
+            both = sb(name, [P, 2 * PACK], F32)
+            nc.vector.tensor_copy(both[:, :PACK], slope[:])
+            nc.vector.scalar_tensor_tensor(both[:, PACK:], slope[:], -1.0, threshold[:], ALU.mult, ALU.mult)
+            return both
 
-        def pick(name, lst, wtag=None, stag=None):
-            w = sb(name + "w", [P, C], U32, wtag)
-            s = sb(name + "s", [P, C], U8, stag)
-            nc.vector.tensor_copy(w[:].rearrange("p (t m) -> p m t", t=PACK), xw[:].indirect(lst[:]))
-            nc.vector.tensor_copy(s[:].rearrange("p (t m) -> p m t", t=PACK), xs[:].indirect(lst[:]))
-            return w, s
+        gate1 = gate_bias("gate1", sl_t, th_t)
+        nb0 = sb("nb0", [P, 1], F32, "y1")
+        nc.vector.tensor_copy(nb0[:], gate1[:, PACK : PACK + 1])
+        sl0 = sb("sl0", [P, 1], F32, "y3")
+        nc.vector.tensor_copy(sl0[:], sl_t[:, :1])
+
+        def pick(name, table, lst, tag=None):
+            picked = sb(name, [P, C], table.dtype, tag)
+            nc.vector.tensor_copy(picked[:].rearrange("p (t m) -> p m t", t=PACK), table[:].indirect(lst[:]))
+            return picked
 
         def mm(out, lhs, t, rhs):
             cols = slice(t * P, (t + 1) * P)
@@ -111,24 +116,28 @@ def tile_picked_tricdqxbgxbehp_none_po_kernel(
                 rhs=rhs[0][:].bitcast(FP8X4), rhs_scale=rhs[1][:], start=True, stop=True,
             )
 
-        st_t, bg_t = [], []
+        st_t, asg_t, bg_t = [], [], []
         for t in range(PACK):
             py = psum.tile([P, S], F32, name=f"pn{t}")
             mm(py[:], (wwd, wsd), t, (xqw, xqs))
-            y = sb(f"y{t}", [P, S], F32)
-            move = nc.scalar.copy if t else nc.vector.tensor_copy
-            move(y[:], py[:])
-            st = sb(f"st{t}", [P, 2 * S], F32)
+            y = sb(f"y{t}", [P, S], F32, "y0" if t == 2 else None)
+            (nc.scalar.copy if t else nc.vector.tensor_copy)(y[:], py[:])
+            st = sb(f"st{t}", [P, S], F32)
+            asg = sb(f"asg{t}", [P, 2 * S], F32)
             for h in range(2):
                 nc.scalar.activation(
-                    st[:, S + h * HALF : S + (h + 1) * HALF], y[:].indirect(half(n1_t, h)), ACT.Sigmoid,
-                    bias=nb1[:, t : t + 1] if t else nb0[:], scale=sl_t[:, t : t + 1],
+                    asg[:, S + h * HALF : S + (h + 1) * HALF], y[:].indirect(half(n1_t, h)), ACT.Sigmoid,
+                    bias=gate1[:, PACK + t : PACK + t + 1] if t else nb0[:], scale=gate1[:, t : t + 1] if t else sl0[:],
                 )
-            nc.vector.scalar_tensor_tensor(st[:, :S], py[:], gs_t[:, t : t + 1], st[:, S:], ALU.mult, ALU.mult)
+            nc.vector.scalar_tensor_tensor(st[:], py[:], gs_t[:, t : t + 1], asg[:, S:], ALU.mult, ALU.mult)
             st_t.append(st)
+            asg_t.append(asg)
             bg_t.append(sb(f"bg{t}", [P, 2 * S], F32))
 
-        xb = pick("xb", cb_t)
+        xb = (pick("xbw", xw, cb_t, "xqw"), pick("xbs", xs, cb_t, "xqs"))
+        xdw = pick("xdw", xw, cd_t, "y1")
+        xaw = pick("xaw", xw, ca_t, "y0")
+        xd = (xdw, pick("xds", xs, cd_t, "gs"))
         zw = sb("zw", [P, S], U32)
         zs = sb("zs", [P, S], U8)
         for h in range(2):
@@ -136,8 +145,8 @@ def tile_picked_tricdqxbgxbehp_none_po_kernel(
             zb = sb(f"zb{h}", [P, PACK, HALF], BF16)
             for t in range(PACK):
                 g = bg_t[t][:, S + h * HALF : S + (h + 1) * HALF]
-                nc.scalar.activation(g, st_t[t][:].indirect(half(n2_t, h)), ACT.Copy)
-                nc.vector.scalar_tensor_tensor(zb[:, t, :], g, -0.5, st_t[t][:, cols], ALU.mult, ALU.add)
+                nc.scalar.activation(g, st_t[t][:].indirect(half(n2_t, h)), ACT.Copy, scale=-0.5)
+                (nc.vector if h else nc.gpsimd).tensor_tensor(zb[:, t, :], g, st_t[t][:, cols], ALU.add)
             zi = sb(f"zi{h}", [P, HALF * PACK], BF16)
             nc.vector.tensor_copy(
                 zi[:].rearrange("p (c i t) -> p c t i", t=PACK, i=4),
@@ -145,68 +154,66 @@ def tile_picked_tricdqxbgxbehp_none_po_kernel(
             )
             nc.vector.quantize_mx(zw[:, cols].bitcast(FP8X4), zs[:, cols], zi[:])
 
-        xd = pick("xd", cd_t, "y1", "y3")
-
+        gate5 = gate_bias("gate5", sl2_t, th2_t)
+        tau_c = sb("tau_c", [P, PACK], F32)
+        nc.vector.tensor_copy(tau_c[:], tau_t[:])
         ea = sb("ea", [P, PACK * S], F32)
-        nb3 = sb("nb3", [P, PACK], F32)
         for t in range(PACK):
             pb = psum.tile([P, S], F32, name=f"pw{t}")
             mm(pb[:], xb, t, (zw, zs))
             top = sb(f"top{t}", [P, 1], F32)
             nc.vector.tensor_scalar(bg_t[t][:, :S], pb[:], 0.0625, None, ALU.mult, ALU.max, accum_out=top[:])
-            nc.vector.tensor_scalar(nb3[:, t : t + 1], top[:], tau_t[:, t : t + 1], -1.0, ALU.mult, ALU.mult)
+            nb3 = sb(f"nb3{t}", [P, 1], F32)
+            nc.vector.tensor_scalar(nb3[:], top[:], tau_t[:, t : t + 1], -1.0, ALU.mult, ALU.mult)
             nc.scalar.activation(
                 ea[:, t * S : (t + 1) * S], bg_t[t][:].indirect(n3_t[:]), ACT.Exp,
-                bias=nb3[:, t : t + 1], scale=tau_t[:, t : t + 1],
+                bias=nb3[:], scale=tau_c[:, t : t + 1],
             )
-        xa = pick("xa", ca_t, "zi1", "top3")
-        nb5 = sb("nb5", [P, PACK], F32)
-        nc.vector.scalar_tensor_tensor(nb5[:], sl2_t[:], -1.0, th2_t[:], ALU.mult, ALU.mult)
-
-        rs = sb("rs", [P, PACK * S], F32)
-        nc.scalar.activation(rs[:], ea[:], ACT.Abs_reciprocal_sqrt, bias=0.25)
-
         for t in range(PACK):
-            pq = psum.tile([P, S], F32, name=f"pn{t}")
+            pq = psum.tile([P, S], F32, name=f"pw{t}")
             mm(pq[:], xd, t, (zw, zs))
             nc.scalar.activation(bg_t[t][:, :S], pq[:], ACT.Copy, scale=0.0625)
+        rs = sb("rs", [P, PACK * S], F32, "nb33")
+        for h in range(2):
+            cols = slice(2 * h * S, 2 * (h + 1) * S)
+            nc.scalar.activation(rs[:, cols], ea[:, cols], ACT.Abs_reciprocal_sqrt, bias=0.25)
 
-        d_t = []
+        xa = (xaw, pick("xas", xs, ca_t, "top3"))
+        md_t = []
         for t in range(PACK):
-            pa = psum.tile([P, S], F32, name=f"pw{t}")
+            pa = psum.tile([P, S], F32, name=f"pn{t}")
             mm(pa[:], xa, t, (zw, zs))
-            nc.vector.tensor_scalar(st_t[t][:, :S], pa[:], 0.0625, None, ALU.mult)
+            nc.vector.tensor_scalar(asg_t[t][:, :S], pa[:], 0.0625, None, ALU.mult)
             ga = sb(f"ga{t}", [P, S], F32)
-            nc.vector.tensor_copy(ga[:], st_t[t][:].indirect(n4_t[:]))
-            d = sb(f"d{t}", [P, S], F32)
-            nc.vector.scalar_tensor_tensor(d[:], pa[:], 0.0625, ga[:], ALU.mult, ALU.subtract)
-            d_t.append(d)
+            nc.vector.tensor_copy(ga[:], asg_t[t][:].indirect(n4_t[:]))
+            md = sb(f"md{t}", [P, 2 * S], F32)
+            nc.gpsimd.tensor_tensor(md[:, S:], asg_t[t][:, :S], ga[:], ALU.subtract)
+            md_t.append(md)
+
         for t in range(PACK):
             cols = slice(t * S, (t + 1) * S)
             nc.scalar.activation(
                 ea[:, cols], bg_t[t][:].indirect(n5_t[:]), ACT.Sigmoid,
-                bias=nb5[:, t : t + 1], scale=sl2_t[:, t : t + 1],
+                bias=gate5[:, PACK + t : PACK + t + 1], scale=gate5[:, t : t + 1],
             )
-        hm_t = []
+        g6_t = []
         for t in range(PACK):
             cols = slice(t * S, (t + 1) * S)
-            hm = sb(f"hm{t}", [P, 2 * S], F32)
-            nc.vector.scalar_tensor_tensor(hm[:, S:], d_t[t][:], -0.25, rs[:, cols], ALU.mult, ALU.mult)
-            nc.vector.tensor_tensor(hm[:, :S], hm[:, S:], rs[:, cols], ALU.mult)
-            hm_t.append(hm)
+            md = md_t[t]
+            rec = sb(f"rec{t}", [P, S], F32)
+            nc.gpsimd.tensor_tensor(rec[:], rs[:, cols], rs[:, cols], ALU.mult)
+            nc.vector.scalar_tensor_tensor(md[:, :S], md[:, S:], 0.5, rec[:], ALU.mult, ALU.mult)
+            g6 = sb(f"g6{t}", [P, S], F32)
+            nc.vector.tensor_copy(g6[:], md[:].indirect(n6_t[:]))
+            g6_t.append(g6)
 
         o = sb("o", [P, PACK, S], F32)
         out_rows = out_0.rearrange("(p t) j -> p t j", t=PACK)
         for t in range(PACK):
             cols = slice(t * S, (t + 1) * S)
             p = sb(f"p{t}", [P, S], F32)
-            nc.vector.scalar_tensor_tensor(p[:], hm_t[t][:, :S], -2.0, ea[:, cols], ALU.mult, ALU.mult)
-            if t < 2:
-                g6 = sb(f"g6{t}", [P, S], F32)
-                nc.scalar.activation(g6[:], hm_t[t][:].indirect(n6_t[:]), ACT.Copy)
-                nc.vector.tensor_tensor(o[:, t, :], g6[:], p[:], ALU.add)
-            else:
-                nc.vector.tensor_tensor(o[:, t, :], hm_t[t][:].indirect(n6_t[:]), p[:], ALU.add)
+            nc.gpsimd.tensor_tensor(p[:], md_t[t][:, :S], ea[:, cols], ALU.mult)
+            nc.vector.scalar_tensor_tensor(o[:, t, :], g6_t[t][:], -0.5, p[:], ALU.mult, ALU.add)
             nc.sync.dma_start(out_rows[:, t, :], o[:, t, :])
 
         ow = sb("ow", [P, S], U32)

@@ -60,11 +60,11 @@ def tile_picked_tricdqxbgxbehp_none_po_kernel(
         nc.sync.dma_start(xw[:].bitcast(I32), x_words[0].rearrange("p n r -> p (n r)").bitcast(I32))
         load_scales(ws, w1_scales, [nc.scalar] * 3 + [nc.gpsimd])
         load_scales(xs, x_scales, [nc.scalar] * 4)
-        nc.sync.dma_start(ww[:].bitcast(I32), w1_words[0].rearrange("p n r -> p (n r)").bitcast(I32))
-        n1_t = load_list("n1", n1)
         sl_t = load_rows("sl", sl, nc.sync)
+        nc.sync.dma_start(ww[:].bitcast(I32), w1_words[0].rearrange("p n r -> p (n r)").bitcast(I32))
         th_t = load_rows("th", th, nc.sync)
         cb_t = load_list("cb", cb)
+        n1_t = load_list("n1", n1)
         gs_t = load_rows("gs", gs, nc.gpsimd)
         cd_t = load_list("cd", cd)
         ca_t = load_list("ca", ca)
@@ -88,21 +88,20 @@ def tile_picked_tricdqxbgxbehp_none_po_kernel(
         nc.vector.tensor_copy(xqs[:], xs[:].indirect(offs_t[:]))
 
         wwd = sb("wwd", [P, H], U32)
-        nc.vector.tensor_copy(
+        warm = sb("warm", [P, 1], F32)
+        nc.scalar.activation(warm[:], sl_t[:, :1], ACT.Sigmoid)
+        nc.scalar.copy(
             wwd[:].rearrange("p (t g i) -> p g t i", t=PACK, i=4),
             ww[:].rearrange("p (g i t) -> p g t i", t=PACK, i=4),
         )
         def gate_bias(name, slope, threshold):
-            both = sb(name, [P, 2 * PACK], F32)
-            nc.vector.tensor_copy(both[:, :PACK], slope[:])
-            nc.vector.scalar_tensor_tensor(both[:, PACK:], slope[:], -1.0, threshold[:], ALU.mult, ALU.mult)
-            return both
+            neg = sb(name + "n", [P, PACK], F32)
+            nc.gpsimd.tensor_scalar(neg[:], threshold[:], -1.0, 0.0, ALU.mult, ALU.add)
+            bias = sb(name, [P, PACK], F32)
+            nc.gpsimd.tensor_tensor(bias[:], slope[:], neg[:], ALU.mult)
+            return bias
 
-        gate1 = gate_bias("gate1", sl_t, th_t)
-        nb0 = sb("nb0", [P, 1], F32, "y1")
-        nc.vector.tensor_copy(nb0[:], gate1[:, PACK : PACK + 1])
-        sl0 = sb("sl0", [P, 1], F32, "y3")
-        nc.vector.tensor_copy(sl0[:], sl_t[:, :1])
+        nb1 = gate_bias("nb1", sl_t, th_t)
 
         def pick(name, table, lst, tag=None):
             picked = sb(name, [P, C], table.dtype, tag)
@@ -120,24 +119,28 @@ def tile_picked_tricdqxbgxbehp_none_po_kernel(
         for t in range(PACK):
             py = psum.tile([P, S], F32, name=f"pn{t}")
             mm(py[:], (wwd, wsd), t, (xqw, xqs))
-            y = sb(f"y{t}", [P, S], F32, "y0" if t == 2 else None)
-            (nc.scalar.copy if t else nc.vector.tensor_copy)(y[:], py[:])
+            y = sb(f"y{t}", [P, S], F32)
+            nc.scalar.copy(y[:], py[:])
             st = sb(f"st{t}", [P, S], F32)
             asg = sb(f"asg{t}", [P, 2 * S], F32)
             for h in range(2):
                 nc.scalar.activation(
                     asg[:, S + h * HALF : S + (h + 1) * HALF], y[:].indirect(half(n1_t, h)), ACT.Sigmoid,
-                    bias=gate1[:, PACK + t : PACK + t + 1] if t else nb0[:], scale=gate1[:, t : t + 1] if t else sl0[:],
+                    bias=nb1[:, t : t + 1], scale=sl_t[:, t : t + 1],
                 )
-            nc.vector.scalar_tensor_tensor(st[:], py[:], gs_t[:, t : t + 1], asg[:, S:], ALU.mult, ALU.mult)
+            if t < 2:
+                ysg = sb(f"ysg{t}", [P, S], F32)
+                nc.gpsimd.tensor_tensor(ysg[:], y[:], asg[:, S:], ALU.mult)
+                nc.gpsimd.tensor_scalar(st[:], ysg[:], gs_t[:, t : t + 1], 0.0, ALU.mult, ALU.add)
+            else:
+                nc.vector.scalar_tensor_tensor(st[:], py[:], gs_t[:, t : t + 1], asg[:, S:], ALU.mult, ALU.mult)
             st_t.append(st)
             asg_t.append(asg)
             bg_t.append(sb(f"bg{t}", [P, 2 * S], F32))
 
-        xb = (pick("xbw", xw, cb_t, "xqw"), pick("xbs", xs, cb_t, "xqs"))
-        xdw = pick("xdw", xw, cd_t, "y1")
-        xaw = pick("xaw", xw, ca_t, "y0")
-        xd = (xdw, pick("xds", xs, cd_t, "gs"))
+        xb = (pick("xbw", xw, cb_t), pick("xbs", xs, cb_t))
+        xd = (pick("xdw", xw, cd_t), pick("xds", xs, cd_t))
+        xa = (pick("xaw", xw, ca_t), pick("xas", xs, ca_t, "gs"))
         zw = sb("zw", [P, S], U32)
         zs = sb("zs", [P, S], U8)
         for h in range(2):
@@ -154,7 +157,7 @@ def tile_picked_tricdqxbgxbehp_none_po_kernel(
             )
             nc.vector.quantize_mx(zw[:, cols].bitcast(FP8X4), zs[:, cols], zi[:])
 
-        gate5 = gate_bias("gate5", sl2_t, th2_t)
+        nb5 = gate_bias("nb5", sl2_t, th2_t)
         tau_c = sb("tau_c", [P, PACK], F32)
         nc.vector.tensor_copy(tau_c[:], tau_t[:])
         ea = sb("ea", [P, PACK * S], F32)
@@ -169,16 +172,11 @@ def tile_picked_tricdqxbgxbehp_none_po_kernel(
                 ea[:, t * S : (t + 1) * S], bg_t[t][:].indirect(n3_t[:]), ACT.Exp,
                 bias=nb3[:], scale=tau_c[:, t : t + 1],
             )
-        for t in range(PACK):
-            pq = psum.tile([P, S], F32, name=f"pw{t}")
-            mm(pq[:], xd, t, (zw, zs))
-            nc.scalar.activation(bg_t[t][:, :S], pq[:], ACT.Copy, scale=0.0625)
         rs = sb("rs", [P, PACK * S], F32, "nb33")
         for h in range(2):
             cols = slice(2 * h * S, 2 * (h + 1) * S)
             nc.scalar.activation(rs[:, cols], ea[:, cols], ACT.Abs_reciprocal_sqrt, bias=0.25)
 
-        xa = (xaw, pick("xas", xs, ca_t, "top3"))
         md_t = []
         for t in range(PACK):
             pa = psum.tile([P, S], F32, name=f"pn{t}")
@@ -191,20 +189,31 @@ def tile_picked_tricdqxbgxbehp_none_po_kernel(
             md_t.append(md)
 
         for t in range(PACK):
+            pq = psum.tile([P, S], F32, name=f"pw{t}")
+            mm(pq[:], xd, t, (zw, zs))
+            if t < 1:
+                nc.scalar.activation(bg_t[t][:, :S], pq[:], ACT.Copy, scale=0.0625)
+            else:
+                nc.vector.tensor_scalar(bg_t[t][:, :S], pq[:], 0.0625, None, ALU.mult)
+        for t in range(PACK):
             cols = slice(t * S, (t + 1) * S)
             nc.scalar.activation(
                 ea[:, cols], bg_t[t][:].indirect(n5_t[:]), ACT.Sigmoid,
-                bias=gate5[:, PACK + t : PACK + t + 1], scale=gate5[:, t : t + 1],
+                bias=nb5[:, t : t + 1], scale=sl2_t[:, t : t + 1],
             )
         g6_t = []
         for t in range(PACK):
             cols = slice(t * S, (t + 1) * S)
             md = md_t[t]
             rec = sb(f"rec{t}", [P, S], F32)
-            nc.gpsimd.tensor_tensor(rec[:], rs[:, cols], rs[:, cols], ALU.mult)
-            nc.vector.scalar_tensor_tensor(md[:, :S], md[:, S:], 0.5, rec[:], ALU.mult, ALU.mult)
+            nc.vector.scalar_tensor_tensor(rec[:], md[:, S:], 0.5, rs[:, cols], ALU.mult, ALU.mult)
+            nc.vector.tensor_tensor(md[:, :S], rec[:], rs[:, cols], ALU.mult)
+        for t in range(PACK):
             g6 = sb(f"g6{t}", [P, S], F32)
-            nc.vector.tensor_copy(g6[:], md[:].indirect(n6_t[:]))
+            if t < 2:
+                nc.vector.tensor_copy(g6[:], md_t[t][:].indirect(n6_t[:]))
+            else:
+                nc.scalar.activation(g6[:], md_t[t][:].indirect(n6_t[:]), ACT.Copy)
             g6_t.append(g6)
 
         o = sb("o", [P, PACK, S], F32)
@@ -212,7 +221,7 @@ def tile_picked_tricdqxbgxbehp_none_po_kernel(
         for t in range(PACK):
             cols = slice(t * S, (t + 1) * S)
             p = sb(f"p{t}", [P, S], F32)
-            nc.gpsimd.tensor_tensor(p[:], md_t[t][:, :S], ea[:, cols], ALU.mult)
+            nc.vector.tensor_tensor(p[:], md_t[t][:, :S], ea[:, cols], ALU.mult)
             nc.vector.scalar_tensor_tensor(o[:, t, :], g6_t[t][:], -0.5, p[:], ALU.mult, ALU.add)
             nc.sync.dma_start(out_rows[:, t, :], o[:, t, :])
 

@@ -18,7 +18,6 @@ ALU = mybir.AluOpType
 P = 128
 PACK = 4
 HALF = S // 2
-HALF_LIST = HALF // 16
 
 
 def tile_picked_tricdqxbgxbehp_none_po_kernel(
@@ -47,9 +46,6 @@ def tile_picked_tricdqxbgxbehp_none_po_kernel(
             for q, eng in enumerate(engs):
                 eng.dma_start(t[32 * q : 32 * q + 4, :].bitcast(I32), src[0, 4 * q : 4 * q + 4, :].bitcast(I32))
 
-        def half(t, h):
-            return t[:, h * HALF_LIST : (h + 1) * HALF_LIST]
-
         xw = sb("xw", [P, T], U32)
         xs = sb("xs", [P, T], U8)
         ww = sb("ww", [P, H], U32)
@@ -58,14 +54,14 @@ def tile_picked_tricdqxbgxbehp_none_po_kernel(
         nc.gpsimd.memset(xs[:].bitcast(I32), 0)
         offs_t = load_list("offs", offs)
         nc.sync.dma_start(xw[:].bitcast(I32), x_words[0].rearrange("p n r -> p (n r)").bitcast(I32))
-        load_scales(ws, w1_scales, [nc.scalar] * 3 + [nc.gpsimd])
-        load_scales(xs, x_scales, [nc.scalar] * 4)
+        load_scales(ws, w1_scales, [nc.scalar] * 4)
+        load_scales(xs, x_scales, [nc.scalar] * 3 + [nc.gpsimd])
         sl_t = load_rows("sl", sl, nc.sync)
         nc.sync.dma_start(ww[:].bitcast(I32), w1_words[0].rearrange("p n r -> p (n r)").bitcast(I32))
         th_t = load_rows("th", th, nc.sync)
         cb_t = load_list("cb", cb)
         n1_t = load_list("n1", n1)
-        gs_t = load_rows("gs", gs, nc.gpsimd)
+        gs_t = load_rows("gs", gs, nc.sync)
         cd_t = load_list("cd", cd)
         ca_t = load_list("ca", ca)
         n2_t = load_list("n2", n2)
@@ -115,45 +111,43 @@ def tile_picked_tricdqxbgxbehp_none_po_kernel(
                 rhs=rhs[0][:].bitcast(FP8X4), rhs_scale=rhs[1][:], start=True, stop=True,
             )
 
-        st_t, asg_t, bg_t = [], [], []
+        asg_t, bg_t = [], []
         for t in range(PACK):
             py = psum.tile([P, S], F32, name=f"pn{t}")
             mm(py[:], (wwd, wsd), t, (xqw, xqs))
-            y = sb(f"y{t}", [P, S], F32)
-            nc.scalar.copy(y[:], py[:])
-            st = sb(f"st{t}", [P, S], F32)
+            y = sb(f"y{t}", [P, 2 * S], F32)
+            nc.vector.memset(y[:, S:], 0.0)
+            nc.scalar.copy(y[:, :S], py[:])
             asg = sb(f"asg{t}", [P, 2 * S], F32)
-            for h in range(2):
-                nc.scalar.activation(
-                    asg[:, S + h * HALF : S + (h + 1) * HALF], y[:].indirect(half(n1_t, h)), ACT.Sigmoid,
-                    bias=nb1[:, t : t + 1], scale=sl_t[:, t : t + 1],
-                )
+            nc.scalar.activation(
+                asg[:, S:], y[:].indirect(n1_t[:]), ACT.Sigmoid,
+                bias=nb1[:, t : t + 1], scale=sl_t[:, t : t + 1],
+            )
             if t < 2:
                 ysg = sb(f"ysg{t}", [P, S], F32)
-                nc.gpsimd.tensor_tensor(ysg[:], y[:], asg[:, S:], ALU.mult)
-                nc.gpsimd.tensor_scalar(st[:], ysg[:], gs_t[:, t : t + 1], 0.0, ALU.mult, ALU.add)
+                nc.gpsimd.tensor_tensor(ysg[:], y[:, :S], asg[:, S:], ALU.mult)
+                nc.gpsimd.tensor_scalar(asg[:, :S], ysg[:], gs_t[:, t : t + 1], 0.0, ALU.mult, ALU.add)
             else:
-                nc.vector.scalar_tensor_tensor(st[:], py[:], gs_t[:, t : t + 1], asg[:, S:], ALU.mult, ALU.mult)
-            st_t.append(st)
+                nc.vector.scalar_tensor_tensor(asg[:, :S], py[:], gs_t[:, t : t + 1], asg[:, S:], ALU.mult, ALU.mult)
             asg_t.append(asg)
             bg_t.append(sb(f"bg{t}", [P, 2 * S], F32))
 
         xb = (pick("xbw", xw, cb_t), pick("xbs", xs, cb_t))
         xd = (pick("xdw", xw, cd_t), pick("xds", xs, cd_t))
         xa = (pick("xaw", xw, ca_t), pick("xas", xs, ca_t, "gs"))
+        zb = sb("zb", [P, PACK, S], BF16)
+        for t in range(PACK):
+            nc.scalar.activation(bg_t[t][:, S:], asg_t[t][:].indirect(n2_t[:]), ACT.Copy, scale=-0.5)
+            eng = nc.gpsimd if t < 3 else nc.vector
+            eng.tensor_tensor(zb[:, t, :], bg_t[t][:, S:], asg_t[t][:, :S], ALU.add)
         zw = sb("zw", [P, S], U32)
         zs = sb("zs", [P, S], U8)
         for h in range(2):
             cols = slice(h * HALF, (h + 1) * HALF)
-            zb = sb(f"zb{h}", [P, PACK, HALF], BF16)
-            for t in range(PACK):
-                g = bg_t[t][:, S + h * HALF : S + (h + 1) * HALF]
-                nc.scalar.activation(g, st_t[t][:].indirect(half(n2_t, h)), ACT.Copy, scale=-0.5)
-                (nc.vector if h else nc.gpsimd).tensor_tensor(zb[:, t, :], g, st_t[t][:, cols], ALU.add)
             zi = sb(f"zi{h}", [P, HALF * PACK], BF16)
-            nc.vector.tensor_copy(
+            (nc.scalar.copy if h else nc.vector.tensor_copy)(
                 zi[:].rearrange("p (c i t) -> p c t i", t=PACK, i=4),
-                zb[:].rearrange("p t (c i) -> p c t i", i=4),
+                zb[:, :, cols].rearrange("p t (c i) -> p c t i", i=4),
             )
             nc.vector.quantize_mx(zw[:, cols].bitcast(FP8X4), zs[:, cols], zi[:])
 
@@ -201,28 +195,25 @@ def tile_picked_tricdqxbgxbehp_none_po_kernel(
                 ea[:, cols], bg_t[t][:].indirect(n5_t[:]), ACT.Sigmoid,
                 bias=nb5[:, t : t + 1], scale=sl2_t[:, t : t + 1],
             )
-        g6_t = []
         for t in range(PACK):
             cols = slice(t * S, (t + 1) * S)
             md = md_t[t]
             rec = sb(f"rec{t}", [P, S], F32)
-            nc.vector.scalar_tensor_tensor(rec[:], md[:, S:], 0.5, rs[:, cols], ALU.mult, ALU.mult)
+            nc.vector.scalar_tensor_tensor(rec[:], md[:, S:], -0.25, rs[:, cols], ALU.mult, ALU.mult)
             nc.vector.tensor_tensor(md[:, :S], rec[:], rs[:, cols], ALU.mult)
-        for t in range(PACK):
-            g6 = sb(f"g6{t}", [P, S], F32)
-            if t < 2:
-                nc.vector.tensor_copy(g6[:], md_t[t][:].indirect(n6_t[:]))
-            else:
-                nc.scalar.activation(g6[:], md_t[t][:].indirect(n6_t[:]), ACT.Copy)
-            g6_t.append(g6)
 
         o = sb("o", [P, PACK, S], F32)
         out_rows = out_0.rearrange("(p t) j -> p t j", t=PACK)
         for t in range(PACK):
             cols = slice(t * S, (t + 1) * S)
             p = sb(f"p{t}", [P, S], F32)
-            nc.vector.tensor_tensor(p[:], md_t[t][:, :S], ea[:, cols], ALU.mult)
-            nc.vector.scalar_tensor_tensor(o[:, t, :], g6_t[t][:], -0.5, p[:], ALU.mult, ALU.add)
+            nc.vector.scalar_tensor_tensor(p[:], md_t[t][:, :S], -2.0, ea[:, cols], ALU.mult, ALU.mult)
+            if t < 3:
+                nc.vector.tensor_tensor(o[:, t, :], md_t[t][:].indirect(n6_t[:]), p[:], ALU.add)
+            else:
+                g6 = sb(f"g6{t}", [P, S], F32)
+                nc.scalar.activation(g6[:], md_t[t][:].indirect(n6_t[:]), ACT.Copy)
+                nc.vector.tensor_tensor(o[:, t, :], g6[:], p[:], ALU.add)
             nc.sync.dma_start(out_rows[:, t, :], o[:, t, :])
 
         ow = sb("ow", [P, S], U32)
@@ -237,7 +228,7 @@ def tile_picked_tricdqxbgxbehp_none_po_kernel(
                 o[:, :, cols].rearrange("p t (c i) -> p c t i", i=4),
             )
             nc.vector.quantize_mx(ow[:, cols].bitcast(FP8X4), osc[:, cols], oi[:])
-        nc.sync.dma_start(out_words, ow[:].bitcast(I32))
+            nc.sync.dma_start(out_words[:, cols], ow[:, cols].bitcast(I32))
         for q in range(4):
             eng = nc.sync if q % 2 else nc.scalar
             eng.dma_start(out_2[0, 4 * q : 4 * q + 4, :].bitcast(I32), osc[32 * q : 32 * q + 4, :].bitcast(I32))

from contextlib import ExitStack

import concourse.mybir as mybir

K, T, S, H, C = 512, 2048, 256, 512, 512
FLOPS = 2 * K * S * (H + 3 * C)

F32 = mybir.dt.float32
BF16 = mybir.dt.bfloat16
I32 = mybir.dt.int32
U32 = mybir.dt.uint32
U16 = mybir.dt.uint16
U8 = mybir.dt.uint8
FP8X4 = mybir.dt.float8_e4m3fn_x4
ACT = mybir.ActivationFunctionType
ALU = mybir.AluOpType

P = 128
PACK = 4
HALF = S // 2


def tile_picked_tricdqxbgxbehp_none_po_kernel(
    tc, x_words, x_scales, w1_words, w1_scales, sl, th, gs, tau, sl2, th2,
    offs, n1, n2, ca, cb, cd, n3, n4, n5, n6, out_0, out_1, out_2,
):
    nc = tc.nc
    with ExitStack() as ctx:
        pool = ctx.enter_context(tc.tile_pool(name="sb", bufs=1))
        psum = ctx.enter_context(tc.psum_pool(name="ps", bufs=1))

        def sb(name, shape, dtype, tag=None):
            return pool.tile(shape, dtype, name=name, tag=tag or name, align_bytes=64)

        def load_list(name, src):
            t = sb(name, list(src.shape), U16)
            nc.sync.dma_start(t[:], src)
            return t

        def load_rows(name, src, eng):
            t = sb(name, [P, PACK], F32)
            eng.dma_start(t[:], src.rearrange("(p t) o -> p (t o)", t=PACK))
            return t

        def load_scales(t, src, engs):
            for q, eng in enumerate(engs):
                eng.dma_start(t[32 * q : 32 * q + 4, :].bitcast(I32), src[0, 4 * q : 4 * q + 4, :].bitcast(I32))

        xw = sb("xw", [P, T], U32)
        xs = sb("xs", [P, T], U8)
        ww = sb("ww", [P, H], U32)
        ws = sb("ws", [P, H], U8)
        nc.gpsimd.memset(ws[:].bitcast(I32), 0)
        nc.gpsimd.memset(xs[:].bitcast(I32), 0)
        offs_t = load_list("offs", offs)
        nc.sync.dma_start(xw[:].bitcast(I32), x_words[0].rearrange("p n r -> p (n r)").bitcast(I32))
        load_scales(ws, w1_scales, [nc.scalar] * 4)
        load_scales(xs, x_scales, [nc.scalar] * 3 + [nc.gpsimd])
        sl_t = load_rows("sl", sl, nc.sync)
        nc.sync.dma_start(ww[:].bitcast(I32), w1_words[0].rearrange("p n r -> p (n r)").bitcast(I32))
        th_t = load_rows("th", th, nc.sync)
        cb_t = load_list("cb", cb)
        n1_t = load_list("n1", n1)
        gs_t = load_rows("gs", gs, nc.sync)
        cd_t = load_list("cd", cd)
        ca_t = load_list("ca", ca)
        n2_t = load_list("n2", n2)
        tau_t = load_rows("tau", tau, nc.sync)
        sl2_t = load_rows("sl2", sl2, nc.sync)
        th2_t = load_rows("th2", th2, nc.sync)
        n3_t = load_list("n3", n3)
        n4_t = load_list("n4", n4)
        n5_t = load_list("n5", n5)
        n6_t = load_list("n6", n6)

        wsd = sb("wsd", [P, H], U8)
        nc.vector.tensor_copy(
            wsd[:].rearrange("p (t m) -> p m t", t=PACK), ws[:].rearrange("p (m t) -> p m t", t=PACK)
        )

        xqw = sb("xqw", [P, S], U32)
        xqs = sb("xqs", [P, S], U8)
        nc.vector.tensor_copy(xqw[:], xw[:].indirect(offs_t[:]))
        nc.vector.tensor_copy(xqs[:], xs[:].indirect(offs_t[:]))

        wwd = sb("wwd", [P, H], U32)
        warm = sb("warm", [P, 1], F32)
        nc.scalar.activation(warm[:], sl_t[:, :1], ACT.Sigmoid)
        nc.scalar.copy(
            wwd[:].rearrange("p (t g i) -> p g t i", t=PACK, i=4),
            ww[:].rearrange("p (g i t) -> p g t i", t=PACK, i=4),
        )
        def gate_bias(name, slope, threshold):
            neg = sb(name + "n", [P, PACK], F32)
            nc.gpsimd.tensor_scalar(neg[:], threshold[:], -1.0, 0.0, ALU.mult, ALU.add)
            bias = sb(name, [P, PACK], F32)
            nc.gpsimd.tensor_tensor(bias[:], slope[:], neg[:], ALU.mult)
            return bias

        nb1 = gate_bias("nb1", sl_t, th_t)

        def pick(name, table, lst, tag=None):
            picked = sb(name, [P, C], table.dtype, tag)
            nc.vector.tensor_copy(picked[:].rearrange("p (t m) -> p m t", t=PACK), table[:].indirect(lst[:]))
            return picked

        def mm(out, lhs, t, rhs):
            cols = slice(t * P, (t + 1) * P)
            nc.tensor.matmul_mx(
                out, lhsT=lhs[0][:, cols].bitcast(FP8X4), lhsT_scale=lhs[1][:, cols],
                rhs=rhs[0][:].bitcast(FP8X4), rhs_scale=rhs[1][:], start=True, stop=True,
            )

        asg_t, bg_t = [], []
        for t in range(PACK):
            py = psum.tile([P, S], F32, name=f"pn{t}")
            mm(py[:], (wwd, wsd), t, (xqw, xqs))
            y = sb(f"y{t}", [P, 2 * S], F32)
            nc.vector.memset(y[:, S:], 0.0)
            nc.scalar.copy(y[:, :S], py[:])
            asg = sb(f"asg{t}", [P, 2 * S], F32)
            nc.scalar.activation(
                asg[:, S:], y[:].indirect(n1_t[:]), ACT.Sigmoid,
                bias=nb1[:, t : t + 1], scale=sl_t[:, t : t + 1],
            )
            if t < 2:
                ysg = sb(f"ysg{t}", [P, S], F32)
                nc.gpsimd.tensor_tensor(ysg[:], y[:, :S], asg[:, S:], ALU.mult)
                nc.gpsimd.tensor_scalar(asg[:, :S], ysg[:], gs_t[:, t : t + 1], 0.0, ALU.mult, ALU.add)
            else:
                nc.vector.scalar_tensor_tensor(asg[:, :S], py[:], gs_t[:, t : t + 1], asg[:, S:], ALU.mult, ALU.mult)
            asg_t.append(asg)
            bg_t.append(sb(f"bg{t}", [P, 2 * S], F32))

        xb = (pick("xbw", xw, cb_t), pick("xbs", xs, cb_t))
        xd = (pick("xdw", xw, cd_t), pick("xds", xs, cd_t))
        xa = (pick("xaw", xw, ca_t), pick("xas", xs, ca_t, "gs"))
        zb = sb("zb", [P, PACK, S], BF16)
        for t in range(PACK):
            nc.scalar.activation(bg_t[t][:, S:], asg_t[t][:].indirect(n2_t[:]), ACT.Copy, scale=-0.5)
            eng = nc.gpsimd if t < 3 else nc.vector
            eng.tensor_tensor(zb[:, t, :], bg_t[t][:, S:], asg_t[t][:, :S], ALU.add)
        zw = sb("zw", [P, S], U32)
        zs = sb("zs", [P, S], U8)
        for h in range(2):
            cols = slice(h * HALF, (h + 1) * HALF)
            zi = sb(f"zi{h}", [P, HALF * PACK], BF16)
            (nc.scalar.copy if h else nc.vector.tensor_copy)(
                zi[:].rearrange("p (c i t) -> p c t i", t=PACK, i=4),
                zb[:, :, cols].rearrange("p t (c i) -> p c t i", i=4),
            )
            nc.vector.quantize_mx(zw[:, cols].bitcast(FP8X4), zs[:, cols], zi[:])

        nb5 = gate_bias("nb5", sl2_t, th2_t)
        tau_c = sb("tau_c", [P, PACK], F32)
        nc.vector.tensor_copy(tau_c[:], tau_t[:])
        ea = sb("ea", [P, PACK * S], F32)
        for t in range(PACK):
            pb = psum.tile([P, S], F32, name=f"pw{t}")
            mm(pb[:], xb, t, (zw, zs))
            top = sb(f"top{t}", [P, 1], F32)
            nc.vector.tensor_scalar(bg_t[t][:, :S], pb[:], 0.0625, None, ALU.mult, ALU.max, accum_out=top[:])
            nb3 = sb(f"nb3{t}", [P, 1], F32)
            nc.vector.tensor_scalar(nb3[:], top[:], tau_t[:, t : t + 1], -1.0, ALU.mult, ALU.mult)
            nc.scalar.activation(
                ea[:, t * S : (t + 1) * S], bg_t[t][:].indirect(n3_t[:]), ACT.Exp,
                bias=nb3[:], scale=tau_c[:, t : t + 1],
            )
        rs = sb("rs", [P, PACK * S], F32, "nb33")
        for h in range(2):
            cols = slice(2 * h * S, 2 * (h + 1) * S)
            nc.scalar.activation(rs[:, cols], ea[:, cols], ACT.Abs_reciprocal_sqrt, bias=0.25)

        md_t = []
        for t in range(PACK):
            pa = psum.tile([P, S], F32, name=f"pn{t}")
            mm(pa[:], xa, t, (zw, zs))
            nc.vector.tensor_scalar(asg_t[t][:, :S], pa[:], 0.0625, None, ALU.mult)
            ga = sb(f"ga{t}", [P, S], F32)
            nc.vector.tensor_copy(ga[:], asg_t[t][:].indirect(n4_t[:]))
            md = sb(f"md{t}", [P, 2 * S], F32)
            nc.gpsimd.tensor_tensor(md[:, S:], asg_t[t][:, :S], ga[:], ALU.subtract)
            md_t.append(md)

        for t in range(PACK):
            pq = psum.tile([P, S], F32, name=f"pw{t}")
            mm(pq[:], xd, t, (zw, zs))
            if t < 1:
                nc.scalar.activation(bg_t[t][:, :S], pq[:], ACT.Copy, scale=0.0625)
            else:
                nc.vector.tensor_scalar(bg_t[t][:, :S], pq[:], 0.0625, None, ALU.mult)
        for t in range(PACK):
            cols = slice(t * S, (t + 1) * S)
            nc.scalar.activation(
                ea[:, cols], bg_t[t][:].indirect(n5_t[:]), ACT.Sigmoid,
                bias=nb5[:, t : t + 1], scale=sl2_t[:, t : t + 1],
            )
        for t in range(PACK):
            cols = slice(t * S, (t + 1) * S)
            md = md_t[t]
            rec = sb(f"rec{t}", [P, S], F32)
            nc.vector.scalar_tensor_tensor(rec[:], md[:, S:], -0.25, rs[:, cols], ALU.mult, ALU.mult)
            nc.vector.tensor_tensor(md[:, :S], rec[:], rs[:, cols], ALU.mult)

        o = sb("o", [P, PACK, S], F32)
        out_rows = out_0.rearrange("(p t) j -> p t j", t=PACK)
        for t in range(PACK):
            cols = slice(t * S, (t + 1) * S)
            p = sb(f"p{t}", [P, S], F32)
            nc.vector.scalar_tensor_tensor(p[:], md_t[t][:, :S], -2.0, ea[:, cols], ALU.mult, ALU.mult)
            if t < 3:
                nc.vector.tensor_tensor(o[:, t, :], md_t[t][:].indirect(n6_t[:]), p[:], ALU.add)
            else:
                g6 = sb(f"g6{t}", [P, S], F32)
                nc.scalar.activation(g6[:], md_t[t][:].indirect(n6_t[:]), ACT.Copy)
                nc.vector.tensor_tensor(o[:, t, :], g6[:], p[:], ALU.add)
            nc.sync.dma_start(out_rows[:, t, :], o[:, t, :])

        ow = sb("ow", [P, S], U32)
        osc = sb("osc", [P, S], U8)
        out_words = out_1[0].rearrange("p n r -> p (n r)").bitcast(I32)
        for h in range(2):
            cols = slice(h * HALF, (h + 1) * HALF)
            oi = sb(f"oi{h}", [P, HALF * PACK], BF16)
            move = nc.scalar.copy if h else nc.vector.tensor_copy
            move(
                oi[:].rearrange("p (c i t) -> p c t i", t=PACK, i=4),
                o[:, :, cols].rearrange("p t (c i) -> p c t i", i=4),
            )
            nc.vector.quantize_mx(ow[:, cols].bitcast(FP8X4), osc[:, cols], oi[:])
            nc.sync.dma_start(out_words[:, cols], ow[:, cols].bitcast(I32))
        for q in range(4):
            eng = nc.sync if q % 2 else nc.scalar
            eng.dma_start(out_2[0, 4 * q : 4 * q + 4, :].bitcast(I32), osc[32 * q : 32 * q + 4, :].bitcast(I32))
